import numpy as np
import ml_dtypes


def mxq(x, axis, fmt="e4m3"):
    dtype, down = {"e4m3": (ml_dtypes.float8_e4m3fn, 7), "e5m2": (ml_dtypes.float8_e5m2, 14)}[fmt]
    v = np.moveaxis(np.asarray(x, np.float32).astype(ml_dtypes.bfloat16).astype(np.float64), axis, -1)
    blocks = v.reshape(v.shape[:-1] + (-1, 32))
    amax = np.abs(blocks).max(-1, keepdims=True)
    byte = np.maximum(np.where(amax > 0, np.frexp(amax)[1] - 1 + 127, 0) - down, 1)
    scale = np.exp2(byte - 127.0)
    codes = (blocks / scale).astype(np.float32).astype(dtype).astype(np.float64)
    return np.moveaxis((codes * scale).reshape(v.shape), -1, axis)


WIDE = False


def mx_kscale(k):
    if not WIDE:
        return np.ones(k)
    levels = np.array([10, -10, 5, -5, 0])
    if k % 512:
        return np.exp2(np.random.permutation(np.resize(levels, k // 32))).repeat(32)
    a = np.empty((k // 512, 16))
    for p in range(k // 512):
        a[p, :8] = np.random.permutation(np.resize(levels, 8))
        for g in range(8):
            far = levels[np.abs(levels - a[p, g]) >= 10]
            a[p, g + 8] = far[np.random.randint(len(far))]
    return np.exp2(a.ravel()).repeat(32)


def f64(x):
    return np.asarray(x).astype(np.float64)


def striped(idx):
    return np.tile(idx.reshape(-1, 16).T, (8, 1)).astype(np.uint16)


def unstriped(offs):
    return offs[:16].T.reshape(-1).astype(np.int64)


def striped8(idx):
    return np.concatenate([x.reshape(-1, 16).T for x in idx]).astype(np.uint16)


def runs(offs, k):
    lists = np.stack([offs[16 * r : 16 * r + 16].T.reshape(-1) for r in range(8)]).astype(np.int64)
    return lists[np.arange(k) % 512 // 64]


def pack_weight(w):
    k, n = w.shape
    w = f64(np.asarray(w, np.float32).astype(ml_dtypes.bfloat16)).reshape(k // 32, 32, n)
    amax = np.abs(w).max(1)
    byte = np.clip(np.where(amax > 0, np.frexp(amax)[1] - 1 + 127 - 7, 1), 1, 254)
    scaled = (w * np.exp2(127.0 - byte)[:, None, :]).reshape(k, n).astype(np.float32)
    words = np.ascontiguousarray(scaled.reshape(k // 512, 128, 4, n).transpose(0, 1, 3, 2)).astype(ml_dtypes.float8_e4m3fn).view(np.uint8)
    return words, np.ascontiguousarray(byte.astype(np.uint8).reshape(k // 512, 16, n))


def unpack_weight(words, scales):
    g, p, n, _ = words.shape
    vals = np.ascontiguousarray(words).view(ml_dtypes.float8_e4m3fn).astype(np.float64) * np.repeat(np.exp2(scales.astype(np.float64) - 127.0), 8, axis=1)[..., None]
    return vals.transpose(0, 1, 3, 2).reshape(g * 512, n)


K, T, S, N, G, H, W = 512, 1024, 256, 512, 2048, 512, 128


def setup_inputs():
    n = np.random.standard_normal
    s = mx_kscale(K)[:, None]
    u = mx_kscale(K)
    packed_xT = pack_weight(n((K, T)) * s)
    packed_dT = pack_weight(n((K, G)) / s)
    packed_w1 = pack_weight(n((H, N)) / np.sqrt(2 * H) / u[:, None])
    packed_w2 = pack_weight(n((K, N)) / np.sqrt(2 * K) / s)
    perm = np.random.permutation(S)
    perm2 = np.random.permutation(S)
    perm3 = np.random.permutation(S)
    return {
        "x_words": packed_xT[0],
        "x_scales": packed_xT[1],
        "d_words": packed_dT[0],
        "d_scales": packed_dT[1],
        "gn": (np.random.uniform(0.5, 1.5, (H, 1)) * u[:, None]).astype(np.float32),
        "w1_words": packed_w1[0],
        "w1_scales": packed_w1[1],
        "w2_words": packed_w2[0],
        "w2_scales": packed_w2[1],
        "offs": striped(np.random.permutation(T)[:S]),
        "k1": striped8(np.random.randint(0, G, (8, H))),
        "two": striped(np.random.permutation(T)[:S]),
        "k2": striped8(np.random.randint(0, G, (8, H))),
        "n1": striped(perm[:W]),
        "n2": striped(perm[W:]),
        "n3": striped(np.random.permutation(S)),
        "hz": striped8(np.random.randint(0, T, (8, S))),
        "n4": striped(perm2[:W]),
        "n5": striped(perm2[W:]),
        "n6": striped(perm3[:W]),
        "n7": striped(perm3[W:]),
        "n8": striped(np.random.permutation(S)),
    }


def reference(x_words, x_scales, d_words, d_scales, gn, w1_words, w1_scales, w2_words, w2_scales, offs, k1, two, k2, n1, n2, n3, hz, n4, n5, n6, n7, n8):
    d_k1 = unpack_weight(d_words, d_scales)[np.arange(K)[:, None], runs(k1, K)]
    xq = unpack_weight(x_words, x_scales)[:, unstriped(offs)]
    d_k2 = unpack_weight(d_words, d_scales)[np.arange(K)[:, None], runs(k2, K)]
    x_two = unpack_weight(x_words, x_scales)[:, unstriped(two)]
    h = 0.0625 * (d_k1.T @ xq + d_k2.T @ x_two)
    pa = h[:, unstriped(n1)]
    pb = h[:, unstriped(n2)]
    rb = np.minimum(pa, pb)
    ra = np.maximum(pa, pb)
    ua = np.zeros((H, S))
    ua[:, unstriped(n1)] = ra
    ub = ua.copy()
    ub[:, unstriped(n2)] = rb
    z = f64(gn) * (ub - ub[:, unstriped(n3)])
    x_hz = unpack_weight(x_words, x_scales)[np.arange(K)[:, None], runs(hz, K)]
    h2 = unpack_weight(w1_words, w1_scales).T @ mxq(z, 0, "e4m3") + unpack_weight(w2_words, w2_scales).T @ x_hz
    pa2 = h2[:, unstriped(n4)]
    pb2 = h2[:, unstriped(n5)]
    ra2 = pb2 - pa2
    ua2 = np.zeros((N, S))
    ua2[:, unstriped(n6)] = ra2
    ub2 = ua2.copy()
    ub2[:, unstriped(n7)] = pa2
    return np.maximum(ub2, h2[:, unstriped(n8)])

@@ -1,0 +1,241 @@
+from contextlib import ExitStack
+
+import concourse.mybir as mybir
+
+F32 = mybir.dt.float32
+BF16 = mybir.dt.bfloat16
+I32 = mybir.dt.int32
+U32 = mybir.dt.uint32
+U16 = mybir.dt.uint16
+U8 = mybir.dt.uint8
+FP8X4 = mybir.dt.float8_e4m3fn_x4
+ALU = mybir.AluOpType
+COPY = mybir.ActivationFunctionType.Copy
+
+P = 128
+K, T, S, N, G, H, W = 512, 1024, 256, 512, 2048, 512, 128
+FLOPS = 536870912
+
+
+def tile_picked_mttznhorddcphw_none_p_kernel(
+    tc, x_words, x_scales, d_words, d_scales, gn, w1_words, w1_scales, w2_words, w2_scales,
+    offs, k1, two, k2, n1, n2, n3, hz, n4, n5, n6, n7, n8, out,
+):
+    nc = tc.nc
+    with ExitStack() as ctx:
+        lists = ctx.enter_context(tc.tile_pool(name="lists", bufs=1))
+        keep = ctx.enter_context(tc.tile_pool(name="keep", bufs=1))
+        psum = ctx.enter_context(tc.psum_pool(name="psum", bufs=1))
+
+        def load_list(name, src):
+            tile = lists.tile(list(src.shape), U16, name=name)
+            nc.sync.dma_start(tile[:], src)
+            return tile
+
+        def words_of(src):
+            return src[0].rearrange("p n t -> p (n t)").bitcast(I32)
+
+        def sb(name, cols, dtype, tag=None):
+            return keep.tile([P, cols], dtype, name=name, tag=tag or name, align_bytes=64)
+
+        def zeroed(engine, name, cols, tag=None):
+            tile = sb(name, cols, U8, tag)
+            engine.memset(tile[:].bitcast(I32), 0)
+            return tile
+
+        d_sc = zeroed(nc.vector, "d_sc", G)
+        x_sc = zeroed(nc.vector, "x_sc", T)
+        placed = zeroed(nc.gpsimd, "placed", 2 * H + 2 * S)
+        hz_placed = zeroed(nc.gpsimd, "hz_placed", S)
+
+        l_k1 = load_list("l_k1", k1)
+        l_k2 = load_list("l_k2", k2)
+        nc.scalar.dma_start(d_sc[0:P:8, :].bitcast(I32), d_scales[0].bitcast(I32))
+        nc.scalar.dma_start(x_sc[0:P:8, :].bitcast(I32), x_scales[0].bitcast(I32))
+        l_offs = load_list("l_offs", offs)
+        l_two = load_list("l_two", two)
+        x_w = sb("x_w", T, I32)
+        nc.sync.dma_start(x_w[:], words_of(x_words))
+        d_w = sb("d_w", G, I32)
+        nc.sync.dma_start(d_w[:], words_of(d_words))
+        l_n1 = load_list("l_n1", n1)
+        l_n2 = load_list("l_n2", n2)
+        gain_raw = sb("gain_raw", 4, F32)
+        nc.sync.dma_start(gain_raw[:], gn.rearrange("(p t) o -> p (t o)", t=4))
+        gain = sb("gain", 4, F32)
+        nc.scalar.activation(gain[:], gain_raw[:], COPY, scale=0.0625)
+
+        picked_sc = sb("picked_sc", 2 * H + 2 * S, U8)
+        nc.vector.tensor_copy(picked_sc[:, 0:H], d_sc[:].indirect(l_k1[:]))
+        nc.vector.tensor_copy(picked_sc[:, H : 2 * H], d_sc[:].indirect(l_k2[:]))
+        nc.vector.tensor_copy(picked_sc[:, 2 * H : 2 * H + S], x_sc[:].indirect(l_offs[:]))
+        nc.vector.tensor_copy(picked_sc[:, 2 * H + S :], x_sc[:].indirect(l_two[:]))
+
+        def place_rows(dst, src):
+            for s in range(4):
+                nc.sync.dma_start(dst[s:P:32, :].bitcast(I32), src[8 * s : P : 32, :].bitcast(I32))
+
+        place_rows(placed, picked_sc)
+
+        x_picked = sb("x_picked", 2 * S, U32, tag="x_picked")
+        nc.vector.tensor_copy(x_picked[:, 0:S], x_w[:].bitcast(U32).indirect(l_offs[:]))
+        nc.vector.tensor_copy(x_picked[:, S:], x_w[:].bitcast(U32).indirect(l_two[:]))
+        d_picked = sb("d_picked", 2 * H, U32)
+        nc.vector.tensor_copy(d_picked[:, 0:H], d_w[:].bitcast(U32).indirect(l_k1[:]))
+        nc.vector.tensor_copy(d_picked[:, H:], d_w[:].bitcast(U32).indirect(l_k2[:]))
+
+        l_n3 = load_list("l_n3", n3)
+        l_hz = load_list("l_hz", hz)
+        l_n4 = load_list("l_n4", n4)
+        l_n5 = load_list("l_n5", n5)
+        l_n7 = load_list("l_n7", n7)
+        l_n8 = load_list("l_n8", n8)
+        l_n6 = load_list("l_n6", n6)
+
+        def fetch(dst, window, offsets):
+            nc.scalar.activation(dst, window[:].indirect(offsets), COPY)
+
+        def put(window, offsets, src):
+            nc.scalar.activation(window[:].indirect(offsets), src, COPY)
+
+        h = []
+
+        def first_product(t):
+            lw = sb("lw%d" % t, 2 * P, U32)
+            ls = sb("ls%d" % t, 2 * P, U8)
+            nc.vector.tensor_copy(lw[:], d_picked[:, t : 2 * H : 4])
+            nc.vector.tensor_copy(ls[:], placed[:, t : 2 * H : 4])
+            acc = psum.tile([P, S], F32, name="acc%d" % t, tag="bank%d" % t)
+            for a in range(2):
+                nc.tensor.matmul_mx(
+                    out=acc[:],
+                    lhsT=lw[:, a * P : (a + 1) * P].bitcast(FP8X4),
+                    lhsT_scale=ls[:, a * P : (a + 1) * P],
+                    rhs=x_picked[:, a * S : (a + 1) * S].bitcast(FP8X4),
+                    rhs_scale=placed[:, 2 * H + a * S : 2 * H + (a + 1) * S],
+                    start=(a == 0),
+                    stop=(a == 1),
+                )
+            ht = sb("h%d" % t, S, F32)
+            if t == 0:
+                nc.scalar.copy(ht[:], acc[:])
+            else:
+                nc.vector.tensor_copy(ht[:], acc[:])
+            h.append(ht)
+
+        ranked = []
+        ub = []
+        z = sb("z", 4 * S, BF16)
+
+        def pair_up(t):
+            pab = sb("pab%d" % t, S, F32)
+            fetch(pab[:, 0:W], h[t], l_n1[:])
+            fetch(pab[:, W:], h[t], l_n2[:])
+            r = sb("ranked%d" % t, S, F32)
+            nc.vector.tensor_tensor(r[:, 0:W], pab[:, 0:W], pab[:, W:], ALU.max)
+            nc.vector.tensor_tensor(r[:, W:], pab[:, 0:W], pab[:, W:], ALU.min)
+            ranked.append(r)
+            ub.append(sb("ub%d" % t, S, F32))
+
+        def difference(t, c):
+            cols = slice(c * W, (c + 1) * W)
+            other = sb("other%d_%d" % (t, c), W, F32)
+            fetch(other[:], ub[t], l_n3[:, c * 8 : (c + 1) * 8])
+            diff = sb("diff%d_%d" % (t, c), W, F32)
+            nc.vector.tensor_tensor(diff[:], ub[t][:, cols], other[:], ALU.subtract)
+            nc.vector.tensor_scalar(z[:, 4 * c * W + t : 4 * (c + 1) * W : 4], diff[:], gain[:, t : t + 1], None, ALU.mult)
+
+        first_product(0)
+        first_product(1)
+        pair_up(0)
+        first_product(2)
+        pair_up(1)
+        first_product(3)
+
+        w_sc = zeroed(nc.gpsimd, "w_sc", 2 * N, tag="picked_sc")
+        w_w = sb("w_w", 2 * N, I32, tag="d_picked")
+        for a, (words, scales) in enumerate(((w2_words, w2_scales), (w1_words, w1_scales))):
+            for q in range(4):
+                nc.sync.dma_start(
+                    w_sc[32 * q : 32 * q + 4, a * N : (a + 1) * N].bitcast(I32), scales[0, 4 * q : 4 * q + 4, :].bitcast(I32)
+                )
+            nc.sync.dma_start(w_w[:, a * N : (a + 1) * N], words_of(words))
+        hz_picked_sc = sb("hz_picked_sc", S, U8)
+        hz_w = sb("hz_w", S, U32, tag="x_picked")
+        nc.vector.tensor_copy(hz_w[:], x_w[:].bitcast(U32).indirect(l_hz[:]))
+        nc.vector.tensor_copy(hz_picked_sc[:], x_sc[:].indirect(l_hz[:]))
+        place_rows(hz_placed, hz_picked_sc)
+        acc2 = {}
+        for c in range(2):
+            cols = slice(c * W, (c + 1) * W)
+            for m in range(4):
+                acc2[m, c] = psum.tile([P, W], F32, name="acc2_%d_%d" % (m, c), tag="bank%d" % (m + 4 * (1 - c)))
+                nc.tensor.matmul_mx(
+                    out=acc2[m, c][:],
+                    lhsT=w_w[:, m * P : (m + 1) * P].bitcast(FP8X4),
+                    lhsT_scale=w_sc[:, m * P : (m + 1) * P],
+                    rhs=hz_w[:, cols].bitcast(FP8X4),
+                    rhs_scale=hz_placed[:, cols],
+                    start=True,
+                    stop=False,
+                )
+
+        for t in range(4):
+            put(ub[t], l_n1[:], ranked[t][:, 0:W])
+            if t > 0:
+                difference(t - 1, 0)
+            put(ub[t], l_n2[:], ranked[t][:, W:])
+            if t > 0:
+                difference(t - 1, 1)
+            if t + 2 < 4:
+                pair_up(t + 2)
+
+        z_w = sb("z_w", S, U32)
+        z_sc = sb("z_sc", S, U8)
+        h2 = [sb("h2_%d" % m, S, F32) for m in range(4)]
+        for c in range(2):
+            difference(3, c)
+        for c in range(2):
+            cols = slice(c * W, (c + 1) * W)
+            nc.vector.quantize_mx(out=z_w[:, cols].bitcast(FP8X4), scales=z_sc[:, cols], in_=z[:, 4 * c * W : 4 * (c + 1) * W])
+            for m in range(4):
+                nc.tensor.matmul_mx(
+                    out=acc2[m, c][:],
+                    lhsT=w_w[:, N + m * P : N + (m + 1) * P].bitcast(FP8X4),
+                    lhsT_scale=w_sc[:, N + m * P : N + (m + 1) * P],
+                    rhs=z_w[:, cols].bitcast(FP8X4),
+                    rhs_scale=z_sc[:, cols],
+                    start=False,
+                    stop=True,
+                )
+        for m in range(4):
+            for c in range(2):
+                cols = slice(c * W, (c + 1) * W)
+                if m == 0:
+                    nc.scalar.copy(h2[m][:, cols], acc2[m, c][:])
+                else:
+                    nc.vector.tensor_copy(h2[m][:, cols], acc2[m, c][:])
+
+        for m in range(4):
+            pa2 = sb("pa2_%d" % m, W, F32)
+            pb2 = sb("pb2_%d" % m, W, F32)
+            ra2 = sb("ra2_%d" % m, W, F32)
+            ub2 = sb("ub2_%d" % m, S, F32)
+            rival = sb("rival%d" % m, S, F32)
+            res = sb("res%d" % m, S, F32)
+            fetch(pa2[:], h2[m], l_n4[:])
+            fetch(pb2[:], h2[m], l_n5[:])
+            nc.vector.tensor_tensor(ra2[:], pb2[:], pa2[:], ALU.subtract)
+            put(ub2, l_n7[:], pa2[:])
+            fetch(rival[:, 0:W], h2[m], l_n8[:, 0:8])
+            put(ub2, l_n6[:], ra2[:])
+            fetch(rival[:, W:], h2[m], l_n8[:, 8:16])
+            rows = slice(m * P, (m + 1) * P)
+            if m < 3:
+                nc.vector.tensor_tensor(res[:], ub2[:], rival[:], ALU.max)
+                nc.sync.dma_start(out[rows, :], res[:])
+            else:
+                for c in range(2):
+                    cols = slice(c * W, (c + 1) * W)
+                    nc.vector.tensor_tensor(res[:, cols], ub2[:, cols], rival[:, cols], ALU.max)
+                    nc.sync.dma_start(out[rows, cols], res[:, cols])

@@ -25,6 +25,7 @@ def tile_picked_mttznhorddcphw_none_p_kernel(
     with ExitStack() as ctx:
         lists = ctx.enter_context(tc.tile_pool(name="lists", bufs=1))
         keep = ctx.enter_context(tc.tile_pool(name="keep", bufs=1))
+        shared = ctx.enter_context(tc.tile_pool(name="shared", bufs=1))
         psum = ctx.enter_context(tc.psum_pool(name="psum", bufs=1))
 
         def load_list(name, src):
@@ -43,46 +44,61 @@ def tile_picked_mttznhorddcphw_none_p_kernel(
             engine.memset(tile[:].bitcast(I32), 0)
             return tile
 
-        d_sc = zeroed(nc.vector, "d_sc", G)
-        x_sc = zeroed(nc.vector, "x_sc", T)
-        placed = zeroed(nc.gpsimd, "placed", 2 * H + 2 * S)
-        hz_placed = zeroed(nc.gpsimd, "hz_placed", S)
+        d_sc = sb("d_sc", G, U8)
+        x_sc = sb("x_sc", T, U8)
+        for table, cols in ((d_sc, G), (x_sc, T)):
+            nc.gpsimd.memset(table[:, 0 : cols // 2].bitcast(I32), 0)
+            nc.vector.memset(table[:, cols // 2 :].bitcast(I32), 0)
+        placed = [zeroed(nc.vector, "placed0", H + 2 * S), zeroed(nc.vector, "placed1", H)]
+        hz_placed = zeroed(nc.vector, "hz_placed", S)
+
+        def window(name):
+            tile = sb(name, S + 16, F32)
+            nc.gpsimd.memset(tile[:, S:], 0.0)
+            return tile
+
+        rows = [window("rows%d" % t) for t in range(4)]
+        h2 = [window("h2_%d" % m) for m in range(4)]
 
         l_k1 = load_list("l_k1", k1)
+        nc.sync.dma_start(d_sc[0:P:8, :].bitcast(I32), d_scales[0].bitcast(I32))
         l_k2 = load_list("l_k2", k2)
-        nc.scalar.dma_start(d_sc[0:P:8, :].bitcast(I32), d_scales[0].bitcast(I32))
-        nc.scalar.dma_start(x_sc[0:P:8, :].bitcast(I32), x_scales[0].bitcast(I32))
+        nc.sync.dma_start(x_sc[0:P:8, :].bitcast(I32), x_scales[0].bitcast(I32))
         l_offs = load_list("l_offs", offs)
         l_two = load_list("l_two", two)
-        x_w = sb("x_w", T, I32)
-        nc.sync.dma_start(x_w[:], words_of(x_words))
         d_w = sb("d_w", G, I32)
         nc.sync.dma_start(d_w[:], words_of(d_words))
+        x_w = sb("x_w", T, I32)
+        nc.sync.dma_start(x_w[:], words_of(x_words))
         l_n1 = load_list("l_n1", n1)
         l_n2 = load_list("l_n2", n2)
         gain_raw = sb("gain_raw", 4, F32)
         nc.sync.dma_start(gain_raw[:], gn.rearrange("(p t) o -> p (t o)", t=4))
         gain = sb("gain", 4, F32)
-        nc.scalar.activation(gain[:], gain_raw[:], COPY, scale=0.0625)
-
-        picked_sc = sb("picked_sc", 2 * H + 2 * S, U8)
-        nc.vector.tensor_copy(picked_sc[:, 0:H], d_sc[:].indirect(l_k1[:]))
-        nc.vector.tensor_copy(picked_sc[:, H : 2 * H], d_sc[:].indirect(l_k2[:]))
-        nc.vector.tensor_copy(picked_sc[:, 2 * H : 2 * H + S], x_sc[:].indirect(l_offs[:]))
-        nc.vector.tensor_copy(picked_sc[:, 2 * H + S :], x_sc[:].indirect(l_two[:]))
+        nc.scalar.activation(gain[:], gain_raw[:], COPY, scale=-0.0625)
 
         def place_rows(dst, src):
             for s in range(4):
+                queue = nc.sync if s % 2 == 0 else nc.scalar
+                queue.dma_start(dst[s:P:32, :].bitcast(I32), src[8 * s : P : 32, :].bitcast(I32))
+
+        def place_rows_sync(dst, src):
+            for s in range(4):
                 nc.sync.dma_start(dst[s:P:32, :].bitcast(I32), src[8 * s : P : 32, :].bitcast(I32))
 
-        place_rows(placed, picked_sc)
+        HALF = H // 2
 
-        x_picked = sb("x_picked", 2 * S, U32, tag="x_picked")
-        nc.vector.tensor_copy(x_picked[:, 0:S], x_w[:].bitcast(U32).indirect(l_offs[:]))
-        nc.vector.tensor_copy(x_picked[:, S:], x_w[:].bitcast(U32).indirect(l_two[:]))
-        d_picked = sb("d_picked", 2 * H, U32)
-        nc.vector.tensor_copy(d_picked[:, 0:H], d_w[:].bitcast(U32).indirect(l_k1[:]))
-        nc.vector.tensor_copy(d_picked[:, H:], d_w[:].bitcast(U32).indirect(l_k2[:]))
+        def pick_code_scales(u, dst):
+            for a, codes in enumerate((l_k1, l_k2)):
+                nc.vector.tensor_copy(dst[:, a * HALF : (a + 1) * HALF], d_sc[:].indirect(codes[:, 16 * u : 16 * (u + 1)]))
+
+        picked_sc = shared.tile([P, H + 2 * S], U8, name="picked_sc0", offset=0, align_bytes=64)
+        pick_code_scales(0, picked_sc)
+        nc.vector.tensor_copy(picked_sc[:, H : H + S], x_sc[:].indirect(l_offs[:]))
+        nc.vector.tensor_copy(picked_sc[:, H + S :], x_sc[:].indirect(l_two[:]))
+        place_rows(placed[0], picked_sc)
+
+        x_picked = [sb("x_offs", S, U32, tag="x_picked"), shared.tile([P, S], U32, name="x_two", offset=H, align_bytes=64)]
 
         l_n3 = load_list("l_n3", n3)
         l_hz = load_list("l_hz", hz)
@@ -100,142 +116,182 @@ def tile_picked_mttznhorddcphw_none_p_kernel(
 
         h = []
 
-        def first_product(t):
-            lw = sb("lw%d" % t, 2 * P, U32)
-            ls = sb("ls%d" % t, 2 * P, U8)
-            nc.vector.tensor_copy(lw[:], d_picked[:, t : 2 * H : 4])
-            nc.vector.tensor_copy(ls[:], placed[:, t : 2 * H : 4])
-            acc = psum.tile([P, S], F32, name="acc%d" % t, tag="bank%d" % t)
-            for a in range(2):
-                nc.tensor.matmul_mx(
-                    out=acc[:],
-                    lhsT=lw[:, a * P : (a + 1) * P].bitcast(FP8X4),
-                    lhsT_scale=ls[:, a * P : (a + 1) * P],
-                    rhs=x_picked[:, a * S : (a + 1) * S].bitcast(FP8X4),
-                    rhs_scale=placed[:, 2 * H + a * S : 2 * H + (a + 1) * S],
-                    start=(a == 0),
-                    stop=(a == 1),
-                )
-            ht = sb("h%d" % t, S, F32)
-            if t == 0:
-                nc.scalar.copy(ht[:], acc[:])
-            else:
-                nc.vector.tensor_copy(ht[:], acc[:])
-            h.append(ht)
+        lw = {}
 
-        ranked = []
-        ub = []
+        def deal_words(u, a, tag_picked, tag_dealt):
+            picked = sb("d_picked%d_%d" % (u, a), HALF, U32, tag=tag_picked)
+            nc.vector.tensor_copy(picked[:], d_w[:].bitcast(U32).indirect((l_k1, l_k2)[a][:, 16 * u : 16 * (u + 1)]))
+            lw[u, a] = sb("lw%d_%d" % (u, a), HALF, U32, tag=tag_dealt)
+            nc.vector.tensor_copy(
+                lw[u, a][:].rearrange("p (t m) -> p m t", t=4), picked[:].rearrange("p (m t) -> p m t", t=4)
+            )
+
+        dealt_sc = {}
+
+        def deal_scales(u):
+            dealt_sc[u] = sb("ls%d" % u, H, U8, tag="ls%d" % u)
+            nc.vector.tensor_copy(
+                dealt_sc[u][:].rearrange("p (a t m) -> p a m t", a=2, t=4),
+                placed[u][:, 0:H].rearrange("p (a m t) -> p a m t", a=2, t=4),
+            )
+
+        def first_products(u):
+            ls = dealt_sc[u]
+            for e in range(2):
+                t = 2 * u + e
+                acc = psum.tile([P, S], F32, name="acc%d" % t, tag="bank%d" % t)
+                for a in range(2):
+                    nc.tensor.matmul_mx(
+                        out=acc[:],
+                        lhsT=lw[u, a][:, e * P : (e + 1) * P].bitcast(FP8X4),
+                        lhsT_scale=ls[:, a * HALF + e * P : a * HALF + (e + 1) * P],
+                        rhs=x_picked[a][:].bitcast(FP8X4),
+                        rhs_scale=placed[0][:, H + a * S : H + (a + 1) * S],
+                        start=(a == 0),
+                        stop=(a == 1),
+                    )
+                ht = sb("h%d" % t, S, F32, tag="h%d" % t)
+                if t == 0:
+                    nc.scalar.copy(ht[:], acc[:])
+                else:
+                    nc.vector.tensor_copy(ht[:], acc[:])
+                h.append(ht)
+
+        larger = []
+        smaller = []
+        ub = [sb("ub%d" % t, S, F32) for t in range(4)]
         z = sb("z", 4 * S, BF16)
 
-        def pair_up(t):
-            pab = sb("pab%d" % t, S, F32)
-            fetch(pab[:, 0:W], h[t], l_n1[:])
-            fetch(pab[:, W:], h[t], l_n2[:])
-            r = sb("ranked%d" % t, S, F32)
-            nc.vector.tensor_tensor(r[:, 0:W], pab[:, 0:W], pab[:, W:], ALU.max)
-            nc.vector.tensor_tensor(r[:, W:], pab[:, 0:W], pab[:, W:], ALU.min)
-            ranked.append(r)
-            ub.append(sb("ub%d" % t, S, F32))
+        def pair_up(u):
+            pa = sb("pa%d" % u, S, F32)
+            pb = sb("pb%d" % u, S, F32)
+            ra = sb("ra%d" % u, S, F32)
+            rb = sb("rb%d" % u, S, F32)
+            for e in range(2):
+                cols = slice(e * W, (e + 1) * W)
+                fetch(pa[:, cols], h[2 * u + e], l_n1[:])
+                fetch(pb[:, cols], h[2 * u + e], l_n2[:])
+                nc.vector.tensor_tensor(ra[:, cols], pa[:, cols], pb[:, cols], ALU.max)
+                larger.append(ra[:, cols])
+                smaller.append(rb[:, cols])
+            nc.vector.tensor_tensor(rb[:], pa[:], pb[:], ALU.min)
 
-        def difference(t, c):
-            cols = slice(c * W, (c + 1) * W)
-            other = sb("other%d_%d" % (t, c), W, F32)
-            fetch(other[:], ub[t], l_n3[:, c * 8 : (c + 1) * 8])
-            diff = sb("diff%d_%d" % (t, c), W, F32)
-            nc.vector.tensor_tensor(diff[:], ub[t][:, cols], other[:], ALU.subtract)
-            nc.vector.tensor_scalar(z[:, 4 * c * W + t : 4 * (c + 1) * W : 4], diff[:], gain[:, t : t + 1], None, ALU.mult)
+        def rank(u):
+            for values, offsets in ((larger, l_n1), (smaller, l_n2)):
+                for t in (2 * u, 2 * u + 1):
+                    put(ub[t], offsets[:], values[t])
 
-        first_product(0)
-        first_product(1)
+        z32 = sb("z32", 4 * S, F32)
+
+        def difference(t, pieces):
+            scaled = sb("scaled%d" % t, S, F32)
+            nc.vector.tensor_scalar(scaled[:], rows[t][:, 0:S], gain[:, t : t + 1], None, ALU.mult)
+            other = sb("other%d" % t, S, F32)
+            for cols in pieces:
+                fetch(other[:, cols], rows[t], l_n3[:, cols.start // 16 : cols.stop // 16])
+                nc.vector.scalar_tensor_tensor(
+                    z32[:, t * S + cols.start : t * S + cols.stop], other[:, cols], gain[:, t : t + 1], scaled[:, cols],
+                    ALU.mult, ALU.subtract,
+                )
+
+        deal_words(0, 0, "pick_a", "deal_a")
+        deal_words(0, 1, "pick_b", "deal_b")
+        nc.vector.tensor_copy(x_picked[0][:], x_w[:].bitcast(U32).indirect(l_offs[:]))
+        deal_scales(0)
+        nc.vector.tensor_copy(x_picked[1][:], x_w[:].bitcast(U32).indirect(l_two[:]))
+        first_products(0)
+        picked_sc = shared.tile([P, H], U8, name="picked_sc1", offset=0, align_bytes=64)
+        pick_code_scales(1, picked_sc)
+        place_rows_sync(placed[1], picked_sc)
         pair_up(0)
-        first_product(2)
+        deal_words(1, 0, "deal_a", "pick_a")
+        deal_words(1, 1, "h0", "pick_b")
+        deal_scales(1)
+        first_products(1)
+        rank(0)
+        for t in range(4):
+            nc.sync.dma_start(rows[t][0:64, 0:S], ub[t // 2][64 * (t % 2) : 64 * (t % 2) + 64, :])
         pair_up(1)
-        first_product(3)
 
-        w_sc = zeroed(nc.gpsimd, "w_sc", 2 * N, tag="picked_sc")
-        w_w = sb("w_w", 2 * N, I32, tag="d_picked")
+        w_sc = shared.tile([P, 2 * N], U8, name="w_sc", offset=0, align_bytes=64)
+        nc.gpsimd.memset(w_sc[:].bitcast(I32), 0)
+        w_w = sb("w_w", 2 * N, I32, tag="deal_a")
         for a, (words, scales) in enumerate(((w2_words, w2_scales), (w1_words, w1_scales))):
             for q in range(4):
                 nc.sync.dma_start(
                     w_sc[32 * q : 32 * q + 4, a * N : (a + 1) * N].bitcast(I32), scales[0, 4 * q : 4 * q + 4, :].bitcast(I32)
                 )
             nc.sync.dma_start(w_w[:, a * N : (a + 1) * N], words_of(words))
-        hz_picked_sc = sb("hz_picked_sc", S, U8)
+        hz_picked_sc = sb("hz_picked_sc", S, U8, tag="ls1")
         hz_w = sb("hz_w", S, U32, tag="x_picked")
         nc.vector.tensor_copy(hz_w[:], x_w[:].bitcast(U32).indirect(l_hz[:]))
         nc.vector.tensor_copy(hz_picked_sc[:], x_sc[:].indirect(l_hz[:]))
-        place_rows(hz_placed, hz_picked_sc)
-        acc2 = {}
-        for c in range(2):
-            cols = slice(c * W, (c + 1) * W)
-            for m in range(4):
-                acc2[m, c] = psum.tile([P, W], F32, name="acc2_%d_%d" % (m, c), tag="bank%d" % (m + 4 * (1 - c)))
-                nc.tensor.matmul_mx(
-                    out=acc2[m, c][:],
-                    lhsT=w_w[:, m * P : (m + 1) * P].bitcast(FP8X4),
-                    lhsT_scale=w_sc[:, m * P : (m + 1) * P],
-                    rhs=hz_w[:, cols].bitcast(FP8X4),
-                    rhs_scale=hz_placed[:, cols],
-                    start=True,
-                    stop=False,
-                )
+        place_rows_sync(hz_placed, hz_picked_sc)
+        groups = [(0, slice(0, W)), (0, slice(W, S)), (1, slice(0, S)), (2, slice(0, S)), (3, slice(0, S))]
+        acc2 = []
+        for g, (m, cols) in enumerate(groups):
+            acc2.append(psum.tile([P, cols.stop - cols.start], F32, name="acc2_%d" % g, tag="bank%d" % ((g + 4) % 8)))
+            nc.tensor.matmul_mx(
+                out=acc2[g][:],
+                lhsT=w_w[:, m * P : (m + 1) * P].bitcast(FP8X4),
+                lhsT_scale=w_sc[:, m * P : (m + 1) * P],
+                rhs=hz_w[:, cols].bitcast(FP8X4),
+                rhs_scale=hz_placed[:, cols],
+                start=True,
+                stop=False,
+            )
 
-        for t in range(4):
-            put(ub[t], l_n1[:], ranked[t][:, 0:W])
-            if t > 0:
-                difference(t - 1, 0)
-            put(ub[t], l_n2[:], ranked[t][:, W:])
-            if t > 0:
-                difference(t - 1, 1)
-            if t + 2 < 4:
-                pair_up(t + 2)
+        rank(1)
+        for t in (0, 2):
+            nc.sync.dma_start(rows[t][64:P, 0:S], ub[2 + t // 2][0:64, :])
+            nc.vector.tensor_copy(rows[t + 1][64:P, 0:S], ub[2 + t // 2][64:P, :])
+        halves = [slice(0, W), slice(W, S)]
+        for t in (1, 3, 0):
+            difference(t, [slice(0, S)])
 
         z_w = sb("z_w", S, U32)
         z_sc = sb("z_sc", S, U8)
-        h2 = [sb("h2_%d" % m, S, F32) for m in range(4)]
+        difference(2, halves)
         for c in range(2):
-            difference(3, c)
+            nc.vector.tensor_copy(
+                z[:, 4 * c * W : 4 * (c + 1) * W].rearrange("p (j i t) -> p j t i", i=4, t=4),
+                z32[:].rearrange("p (t c j i) -> p c j t i", t=4, c=2, i=4)[:, c],
+            )
         for c in range(2):
             cols = slice(c * W, (c + 1) * W)
             nc.vector.quantize_mx(out=z_w[:, cols].bitcast(FP8X4), scales=z_sc[:, cols], in_=z[:, 4 * c * W : 4 * (c + 1) * W])
-            for m in range(4):
-                nc.tensor.matmul_mx(
-                    out=acc2[m, c][:],
-                    lhsT=w_w[:, N + m * P : N + (m + 1) * P].bitcast(FP8X4),
-                    lhsT_scale=w_sc[:, N + m * P : N + (m + 1) * P],
-                    rhs=z_w[:, cols].bitcast(FP8X4),
-                    rhs_scale=z_sc[:, cols],
-                    start=False,
-                    stop=True,
-                )
-        for m in range(4):
-            for c in range(2):
-                cols = slice(c * W, (c + 1) * W)
-                if m == 0:
-                    nc.scalar.copy(h2[m][:, cols], acc2[m, c][:])
-                else:
-                    nc.vector.tensor_copy(h2[m][:, cols], acc2[m, c][:])
+        for g, (m, cols) in enumerate(groups):
+            nc.tensor.matmul_mx(
+                out=acc2[g][:],
+                lhsT=w_w[:, N + m * P : N + (m + 1) * P].bitcast(FP8X4),
+                lhsT_scale=w_sc[:, N + m * P : N + (m + 1) * P],
+                rhs=z_w[:, cols].bitcast(FP8X4),
+                rhs_scale=z_sc[:, cols],
+                start=False,
+                stop=True,
+            )
+            if g == 1:
+                nc.scalar.copy(h2[m][:, cols], acc2[g][:])
+            else:
+                nc.vector.tensor_copy(h2[m][:, cols], acc2[g][:])
 
         for m in range(4):
-            pa2 = sb("pa2_%d" % m, W, F32)
-            pb2 = sb("pb2_%d" % m, W, F32)
+            pa2 = sb("pa2_%d" % m, W, F32, tag="pa2_%d" % m)
+            pb2 = sb("pb2_%d" % m, W, F32, tag="pb2_%d" % m)
             ra2 = sb("ra2_%d" % m, W, F32)
             ub2 = sb("ub2_%d" % m, S, F32)
-            rival = sb("rival%d" % m, S, F32)
             res = sb("res%d" % m, S, F32)
             fetch(pa2[:], h2[m], l_n4[:])
             fetch(pb2[:], h2[m], l_n5[:])
             nc.vector.tensor_tensor(ra2[:], pb2[:], pa2[:], ALU.subtract)
             put(ub2, l_n7[:], pa2[:])
-            fetch(rival[:, 0:W], h2[m], l_n8[:, 0:8])
-            put(ub2, l_n6[:], ra2[:])
-            fetch(rival[:, W:], h2[m], l_n8[:, 8:16])
-            rows = slice(m * P, (m + 1) * P)
-            if m < 3:
-                nc.vector.tensor_tensor(res[:], ub2[:], rival[:], ALU.max)
-                nc.sync.dma_start(out[rows, :], res[:])
-            else:
-                for c in range(2):
-                    cols = slice(c * W, (c + 1) * W)
-                    nc.vector.tensor_tensor(res[:, cols], ub2[:, cols], rival[:, cols], ALU.max)
-                    nc.sync.dma_start(out[rows, cols], res[:, cols])
+            pieces = [slice(0, S)] if m < 3 else [slice(0, 192), slice(192, S)]
+            rivals = []
+            for i, cols in enumerate(pieces):
+                rivals.append(sb("rival%d_%d" % (m, i), cols.stop - cols.start, F32, tag=("pb2_%d", "pa2_%d")[i] % m))
+                fetch(rivals[i][:], h2[m], l_n8[:, cols.start // 16 : cols.stop // 16])
+                if i == 0:
+                    put(ub2, l_n6[:], ra2[:])
+            for cols, rival in zip(pieces, rivals):
+                nc.vector.tensor_tensor(res[:, cols], ub2[:, cols], rival[:], ALU.max)
+                nc.sync.dma_start(out[m * P : (m + 1) * P, cols], res[:, cols])

@@ -49,7 +49,8 @@ def tile_picked_mttznhorddcphw_none_p_kernel(
         for table, cols in ((d_sc, G), (x_sc, T)):
             nc.gpsimd.memset(table[:, 0 : cols // 2].bitcast(I32), 0)
             nc.vector.memset(table[:, cols // 2 :].bitcast(I32), 0)
-        placed = [zeroed(nc.vector, "placed0", H + 2 * S), zeroed(nc.vector, "placed1", H)]
+        placed = [zeroed(nc.vector, "placed0", H + 2 * S), shared.tile([P, H], U8, name="placed1", offset=2624, align_bytes=64)]
+        nc.vector.memset(placed[1][:].bitcast(I32), 0)
         hz_placed = zeroed(nc.vector, "hz_placed", S)
 
         def window(name):
@@ -92,13 +93,13 @@ def tile_picked_mttznhorddcphw_none_p_kernel(
             for a, codes in enumerate((l_k1, l_k2)):
                 nc.vector.tensor_copy(dst[:, a * HALF : (a + 1) * HALF], d_sc[:].indirect(codes[:, 16 * u : 16 * (u + 1)]))
 
-        picked_sc = shared.tile([P, H + 2 * S], U8, name="picked_sc0", offset=0, align_bytes=64)
+        picked_sc = shared.tile([P, H + 2 * S], U8, name="picked_sc0", offset=1024, align_bytes=64)
         pick_code_scales(0, picked_sc)
         nc.vector.tensor_copy(picked_sc[:, H : H + S], x_sc[:].indirect(l_offs[:]))
         nc.vector.tensor_copy(picked_sc[:, H + S :], x_sc[:].indirect(l_two[:]))
         place_rows(placed[0], picked_sc)
 
-        x_picked = [sb("x_offs", S, U32, tag="x_picked"), shared.tile([P, S], U32, name="x_two", offset=H, align_bytes=64)]
+        x_picked = [sb("x_offs", S, U32, tag="x_picked"), shared.tile([P, S], U32, name="x_two", offset=1600, align_bytes=64)]
 
         l_n3 = load_list("l_n3", n3)
         l_hz = load_list("l_hz", hz)
@@ -200,33 +201,34 @@ def tile_picked_mttznhorddcphw_none_p_kernel(
         deal_scales(0)
         nc.vector.tensor_copy(x_picked[1][:], x_w[:].bitcast(U32).indirect(l_two[:]))
         first_products(0)
-        picked_sc = shared.tile([P, H], U8, name="picked_sc1", offset=0, align_bytes=64)
+        picked_sc = shared.tile([P, H], U8, name="picked_sc1", offset=1088, align_bytes=64)
         pick_code_scales(1, picked_sc)
         place_rows_sync(placed[1], picked_sc)
+        w_sc = shared.tile([P, 2 * N], U8, name="w_sc", offset=64, align_bytes=64)
+        nc.vector.memset(w_sc[:].bitcast(I32), 0)
+        for a, scales in enumerate((w2_scales, w1_scales)):
+            for q in range(4):
+                nc.sync.dma_start(
+                    w_sc[32 * q : 32 * q + 4, a * N : (a + 1) * N].bitcast(I32), scales[0, 4 * q : 4 * q + 4, :].bitcast(I32)
+                )
         pair_up(0)
         deal_words(1, 0, "deal_a", "pick_a")
         deal_words(1, 1, "h0", "pick_b")
         deal_scales(1)
         first_products(1)
         rank(0)
-        for t in range(4):
-            nc.sync.dma_start(rows[t][0:64, 0:S], ub[t // 2][64 * (t % 2) : 64 * (t % 2) + 64, :])
         pair_up(1)
 
-        w_sc = shared.tile([P, 2 * N], U8, name="w_sc", offset=0, align_bytes=64)
-        nc.gpsimd.memset(w_sc[:].bitcast(I32), 0)
         w_w = sb("w_w", 2 * N, I32, tag="deal_a")
-        for a, (words, scales) in enumerate(((w2_words, w2_scales), (w1_words, w1_scales))):
-            for q in range(4):
-                nc.sync.dma_start(
-                    w_sc[32 * q : 32 * q + 4, a * N : (a + 1) * N].bitcast(I32), scales[0, 4 * q : 4 * q + 4, :].bitcast(I32)
-                )
+        for a, words in enumerate((w2_words, w1_words)):
             nc.sync.dma_start(w_w[:, a * N : (a + 1) * N], words_of(words))
-        hz_picked_sc = sb("hz_picked_sc", S, U8, tag="ls1")
-        hz_w = sb("hz_w", S, U32, tag="x_picked")
-        nc.vector.tensor_copy(hz_w[:], x_w[:].bitcast(U32).indirect(l_hz[:]))
+        hz_picked_sc = shared.tile([P, S], U8, name="hz_picked_sc", offset=2624, align_bytes=64)
+        hz_w = shared.tile([P, S], U32, name="hz_w", offset=2880, align_bytes=64)
         nc.vector.tensor_copy(hz_picked_sc[:], x_sc[:].indirect(l_hz[:]))
+        nc.vector.tensor_copy(hz_w[:], x_w[:].bitcast(U32).indirect(l_hz[:]))
         place_rows_sync(hz_placed, hz_picked_sc)
+        for t in range(4):
+            nc.sync.dma_start(rows[t][0:64, 0:S], ub[t // 2][64 * (t % 2) : 64 * (t % 2) + 64, :])
         groups = [(0, slice(0, W)), (0, slice(W, S)), (1, slice(0, S)), (2, slice(0, S)), (3, slice(0, S))]
         acc2 = []
         for g, (m, cols) in enumerate(groups):

from contextlib import ExitStack

import concourse.mybir as mybir

F32 = mybir.dt.float32
BF16 = mybir.dt.bfloat16
I32 = mybir.dt.int32
U32 = mybir.dt.uint32
U16 = mybir.dt.uint16
U8 = mybir.dt.uint8
FP8X4 = mybir.dt.float8_e4m3fn_x4
ALU = mybir.AluOpType
COPY = mybir.ActivationFunctionType.Copy

P = 128
K, T, S, N, G, H, W = 512, 1024, 256, 512, 2048, 512, 128
FLOPS = 536870912


def tile_picked_mttznhorddcphw_none_p_kernel(
    tc, x_words, x_scales, d_words, d_scales, gn, w1_words, w1_scales, w2_words, w2_scales,
    offs, k1, two, k2, n1, n2, n3, hz, n4, n5, n6, n7, n8, out,
):
    nc = tc.nc
    with ExitStack() as ctx:
        lists = ctx.enter_context(tc.tile_pool(name="lists", bufs=1))
        keep = ctx.enter_context(tc.tile_pool(name="keep", bufs=1))
        shared = ctx.enter_context(tc.tile_pool(name="shared", bufs=1))
        psum = ctx.enter_context(tc.psum_pool(name="psum", bufs=1))

        def load_list(name, src):
            tile = lists.tile(list(src.shape), U16, name=name)
            nc.sync.dma_start(tile[:], src)
            return tile

        def words_of(src):
            return src[0].rearrange("p n t -> p (n t)").bitcast(I32)

        def sb(name, cols, dtype, tag=None):
            return keep.tile([P, cols], dtype, name=name, tag=tag or name, align_bytes=64)

        def zeroed(engine, name, cols, tag=None):
            tile = sb(name, cols, U8, tag)
            engine.memset(tile[:].bitcast(I32), 0)
            return tile

        d_sc = sb("d_sc", G, U8)
        x_sc = sb("x_sc", T, U8)
        for table, cols in ((d_sc, G), (x_sc, T)):
            nc.gpsimd.memset(table[:, 0 : cols // 2].bitcast(I32), 0)
            nc.vector.memset(table[:, cols // 2 :].bitcast(I32), 0)
        placed = [zeroed(nc.vector, "placed0", H + 2 * S), shared.tile([P, H], U8, name="placed1", offset=2624, align_bytes=64)]
        nc.vector.memset(placed[1][:].bitcast(I32), 0)
        hz_placed = zeroed(nc.vector, "hz_placed", S)

        def window(name):
            tile = sb(name, S + 16, F32)
            nc.gpsimd.memset(tile[:, S:], 0.0)
            return tile

        rows = [window("rows%d" % t) for t in range(4)]
        h2 = [window("h2_%d" % m) for m in range(4)]

        l_k1 = load_list("l_k1", k1)
        nc.sync.dma_start(d_sc[0:P:8, :].bitcast(I32), d_scales[0].bitcast(I32))
        l_k2 = load_list("l_k2", k2)
        nc.sync.dma_start(x_sc[0:P:8, :].bitcast(I32), x_scales[0].bitcast(I32))
        l_offs = load_list("l_offs", offs)
        l_two = load_list("l_two", two)
        d_w = sb("d_w", G, I32)
        nc.sync.dma_start(d_w[:], words_of(d_words))
        x_w = sb("x_w", T, I32)
        nc.sync.dma_start(x_w[:], words_of(x_words))
        l_n1 = load_list("l_n1", n1)
        l_n2 = load_list("l_n2", n2)
        gain_raw = sb("gain_raw", 4, F32)
        nc.sync.dma_start(gain_raw[:], gn.rearrange("(p t) o -> p (t o)", t=4))
        gain = sb("gain", 4, F32)
        nc.scalar.activation(gain[:], gain_raw[:], COPY, scale=-0.0625)

        def place_rows(dst, src):
            for s in range(4):
                queue = nc.sync if s % 2 == 0 else nc.scalar
                queue.dma_start(dst[s:P:32, :].bitcast(I32), src[8 * s : P : 32, :].bitcast(I32))

        def place_rows_sync(dst, src):
            for s in range(4):
                nc.sync.dma_start(dst[s:P:32, :].bitcast(I32), src[8 * s : P : 32, :].bitcast(I32))

        HALF = H // 2

        def pick_code_scales(u, dst):
            for a, codes in enumerate((l_k1, l_k2)):
                nc.vector.tensor_copy(dst[:, a * HALF : (a + 1) * HALF], d_sc[:].indirect(codes[:, 16 * u : 16 * (u + 1)]))

        picked_sc = shared.tile([P, H + 2 * S], U8, name="picked_sc0", offset=1024, align_bytes=64)
        pick_code_scales(0, picked_sc)
        nc.vector.tensor_copy(picked_sc[:, H : H + S], x_sc[:].indirect(l_offs[:]))
        nc.vector.tensor_copy(picked_sc[:, H + S :], x_sc[:].indirect(l_two[:]))
        place_rows(placed[0], picked_sc)

        x_picked = [sb("x_offs", S, U32, tag="x_picked"), shared.tile([P, S], U32, name="x_two", offset=1600, align_bytes=64)]

        l_n3 = load_list("l_n3", n3)
        l_hz = load_list("l_hz", hz)
        l_n4 = load_list("l_n4", n4)
        l_n5 = load_list("l_n5", n5)
        l_n7 = load_list("l_n7", n7)
        l_n8 = load_list("l_n8", n8)
        l_n6 = load_list("l_n6", n6)

        def fetch(dst, window, offsets):
            nc.scalar.activation(dst, window[:].indirect(offsets), COPY)

        def put(window, offsets, src):
            nc.scalar.activation(window[:].indirect(offsets), src, COPY)

        h = []

        lw = {}

        def deal_words(u, a, tag_picked, tag_dealt):
            picked = sb("d_picked%d_%d" % (u, a), HALF, U32, tag=tag_picked)
            nc.vector.tensor_copy(picked[:], d_w[:].bitcast(U32).indirect((l_k1, l_k2)[a][:, 16 * u : 16 * (u + 1)]))
            lw[u, a] = sb("lw%d_%d" % (u, a), HALF, U32, tag=tag_dealt)
            nc.vector.tensor_copy(
                lw[u, a][:].rearrange("p (t m) -> p m t", t=4), picked[:].rearrange("p (m t) -> p m t", t=4)
            )

        dealt_sc = {}

        def deal_scales(u):
            dealt_sc[u] = sb("ls%d" % u, H, U8, tag="ls%d" % u)
            nc.vector.tensor_copy(
                dealt_sc[u][:].rearrange("p (a t m) -> p a m t", a=2, t=4),
                placed[u][:, 0:H].rearrange("p (a m t) -> p a m t", a=2, t=4),
            )

        def first_products(u):
            ls = dealt_sc[u]
            for e in range(2):
                t = 2 * u + e
                acc = psum.tile([P, S], F32, name="acc%d" % t, tag="bank%d" % t)
                for a in range(2):
                    nc.tensor.matmul_mx(
                        out=acc[:],
                        lhsT=lw[u, a][:, e * P : (e + 1) * P].bitcast(FP8X4),
                        lhsT_scale=ls[:, a * HALF + e * P : a * HALF + (e + 1) * P],
                        rhs=x_picked[a][:].bitcast(FP8X4),
                        rhs_scale=placed[0][:, H + a * S : H + (a + 1) * S],
                        start=(a == 0),
                        stop=(a == 1),
                    )
                ht = sb("h%d" % t, S, F32, tag="h%d" % t)
                if t == 0:
                    nc.scalar.copy(ht[:], acc[:])
                else:
                    nc.vector.tensor_copy(ht[:], acc[:])
                h.append(ht)

        larger = []
        smaller = []
        ub = [sb("ub%d" % t, S, F32) for t in range(4)]
        z = sb("z", 4 * S, BF16)

        def pair_up(u):
            pa = sb("pa%d" % u, S, F32)
            pb = sb("pb%d" % u, S, F32)
            ra = sb("ra%d" % u, S, F32)
            rb = sb("rb%d" % u, S, F32)
            for e in range(2):
                cols = slice(e * W, (e + 1) * W)
                fetch(pa[:, cols], h[2 * u + e], l_n1[:])
                fetch(pb[:, cols], h[2 * u + e], l_n2[:])
                nc.vector.tensor_tensor(ra[:, cols], pa[:, cols], pb[:, cols], ALU.max)
                larger.append(ra[:, cols])
                smaller.append(rb[:, cols])
            nc.vector.tensor_tensor(rb[:], pa[:], pb[:], ALU.min)

        def rank(u):
            for values, offsets in ((larger, l_n1), (smaller, l_n2)):
                for t in (2 * u, 2 * u + 1):
                    put(ub[t], offsets[:], values[t])

        z32 = sb("z32", 4 * S, F32)

        def difference(t, pieces):
            scaled = sb("scaled%d" % t, S, F32)
            nc.vector.tensor_scalar(scaled[:], rows[t][:, 0:S], gain[:, t : t + 1], None, ALU.mult)
            other = sb("other%d" % t, S, F32)
            for cols in pieces:
                fetch(other[:, cols], rows[t], l_n3[:, cols.start // 16 : cols.stop // 16])
                nc.vector.scalar_tensor_tensor(
                    z32[:, t * S + cols.start : t * S + cols.stop], other[:, cols], gain[:, t : t + 1], scaled[:, cols],
                    ALU.mult, ALU.subtract,
                )

        deal_words(0, 0, "pick_a", "deal_a")
        deal_words(0, 1, "pick_b", "deal_b")
        nc.vector.tensor_copy(x_picked[0][:], x_w[:].bitcast(U32).indirect(l_offs[:]))
        deal_scales(0)
        nc.vector.tensor_copy(x_picked[1][:], x_w[:].bitcast(U32).indirect(l_two[:]))
        first_products(0)
        picked_sc = shared.tile([P, H], U8, name="picked_sc1", offset=1088, align_bytes=64)
        pick_code_scales(1, picked_sc)
        place_rows_sync(placed[1], picked_sc)
        w_sc = shared.tile([P, 2 * N], U8, name="w_sc", offset=64, align_bytes=64)
        nc.vector.memset(w_sc[:].bitcast(I32), 0)
        for a, scales in enumerate((w2_scales, w1_scales)):
            for q in range(4):
                nc.sync.dma_start(
                    w_sc[32 * q : 32 * q + 4, a * N : (a + 1) * N].bitcast(I32), scales[0, 4 * q : 4 * q + 4, :].bitcast(I32)
                )
        pair_up(0)
        deal_words(1, 0, "deal_a", "pick_a")
        deal_words(1, 1, "h0", "pick_b")
        deal_scales(1)
        first_products(1)
        rank(0)
        pair_up(1)

        w_w = sb("w_w", 2 * N, I32, tag="deal_a")
        for a, words in enumerate((w2_words, w1_words)):
            nc.sync.dma_start(w_w[:, a * N : (a + 1) * N], words_of(words))
        hz_picked_sc = shared.tile([P, S], U8, name="hz_picked_sc", offset=2624, align_bytes=64)
        hz_w = shared.tile([P, S], U32, name="hz_w", offset=2880, align_bytes=64)
        nc.vector.tensor_copy(hz_picked_sc[:], x_sc[:].indirect(l_hz[:]))
        nc.vector.tensor_copy(hz_w[:], x_w[:].bitcast(U32).indirect(l_hz[:]))
        place_rows_sync(hz_placed, hz_picked_sc)
        for t in range(4):
            nc.sync.dma_start(rows[t][0:64, 0:S], ub[t // 2][64 * (t % 2) : 64 * (t % 2) + 64, :])
        groups = [(0, slice(0, W)), (0, slice(W, S)), (1, slice(0, S)), (2, slice(0, S)), (3, slice(0, S))]
        acc2 = []
        for g, (m, cols) in enumerate(groups):
            acc2.append(psum.tile([P, cols.stop - cols.start], F32, name="acc2_%d" % g, tag="bank%d" % ((g + 4) % 8)))
            nc.tensor.matmul_mx(
                out=acc2[g][:],
                lhsT=w_w[:, m * P : (m + 1) * P].bitcast(FP8X4),
                lhsT_scale=w_sc[:, m * P : (m + 1) * P],
                rhs=hz_w[:, cols].bitcast(FP8X4),
                rhs_scale=hz_placed[:, cols],
                start=True,
                stop=False,
            )

        rank(1)
        for t in (0, 2):
            nc.sync.dma_start(rows[t][64:P, 0:S], ub[2 + t // 2][0:64, :])
            nc.vector.tensor_copy(rows[t + 1][64:P, 0:S], ub[2 + t // 2][64:P, :])
        halves = [slice(0, W), slice(W, S)]
        for t in (1, 3, 0):
            difference(t, [slice(0, S)])

        z_w = sb("z_w", S, U32)
        z_sc = sb("z_sc", S, U8)
        difference(2, halves)
        for c in range(2):
            nc.vector.tensor_copy(
                z[:, 4 * c * W : 4 * (c + 1) * W].rearrange("p (j i t) -> p j t i", i=4, t=4),
                z32[:].rearrange("p (t c j i) -> p c j t i", t=4, c=2, i=4)[:, c],
            )
        for c in range(2):
            cols = slice(c * W, (c + 1) * W)
            nc.vector.quantize_mx(out=z_w[:, cols].bitcast(FP8X4), scales=z_sc[:, cols], in_=z[:, 4 * c * W : 4 * (c + 1) * W])
        for g, (m, cols) in enumerate(groups):
            nc.tensor.matmul_mx(
                out=acc2[g][:],
                lhsT=w_w[:, N + m * P : N + (m + 1) * P].bitcast(FP8X4),
                lhsT_scale=w_sc[:, N + m * P : N + (m + 1) * P],
                rhs=z_w[:, cols].bitcast(FP8X4),
                rhs_scale=z_sc[:, cols],
                start=False,
                stop=True,
            )
            if g == 1:
                nc.scalar.copy(h2[m][:, cols], acc2[g][:])
            else:
                nc.vector.tensor_copy(h2[m][:, cols], acc2[g][:])

        for m in range(4):
            pa2 = sb("pa2_%d" % m, W, F32, tag="pa2_%d" % m)
            pb2 = sb("pb2_%d" % m, W, F32, tag="pb2_%d" % m)
            ra2 = sb("ra2_%d" % m, W, F32)
            ub2 = sb("ub2_%d" % m, S, F32)
            res = sb("res%d" % m, S, F32)
            fetch(pa2[:], h2[m], l_n4[:])
            fetch(pb2[:], h2[m], l_n5[:])
            nc.vector.tensor_tensor(ra2[:], pb2[:], pa2[:], ALU.subtract)
            put(ub2, l_n7[:], pa2[:])
            pieces = [slice(0, S)] if m < 3 else [slice(0, 192), slice(192, S)]
            rivals = []
            for i, cols in enumerate(pieces):
                rivals.append(sb("rival%d_%d" % (m, i), cols.stop - cols.start, F32, tag=("pb2_%d", "pa2_%d")[i] % m))
                fetch(rivals[i][:], h2[m], l_n8[:, cols.start // 16 : cols.stop // 16])
                if i == 0:
                    put(ub2, l_n6[:], ra2[:])
            for cols, rival in zip(pieces, rivals):
                nc.vector.tensor_tensor(res[:, cols], ub2[:, cols], rival[:], ALU.max)
                nc.sync.dma_start(out[m * P : (m + 1) * P, cols], res[:, cols])
